import numpy as np
import ml_dtypes


def mxq(x, axis, fmt="e4m3"):
    dtype, down = {"e4m3": (ml_dtypes.float8_e4m3fn, 7), "e5m2": (ml_dtypes.float8_e5m2, 14)}[fmt]
    v = np.moveaxis(np.asarray(x, np.float32).astype(ml_dtypes.bfloat16).astype(np.float64), axis, -1)
    blocks = v.reshape(v.shape[:-1] + (-1, 32))
    amax = np.abs(blocks).max(-1, keepdims=True)
    byte = np.maximum(np.where(amax > 0, np.frexp(amax)[1] - 1 + 127, 0) - down, 1)
    scale = np.exp2(byte - 127.0)
    codes = (blocks / scale).astype(np.float32).astype(dtype).astype(np.float64)
    return np.moveaxis((codes * scale).reshape(v.shape), -1, axis)


WIDE = False


def mx_kscale(k):
    if not WIDE:
        return np.ones(k)
    levels = np.array([10, -10, 5, -5, 0])
    if k % 512:
        return np.exp2(np.random.permutation(np.resize(levels, k // 32))).repeat(32)
    a = np.empty((k // 512, 16))
    for p in range(k // 512):
        a[p, :8] = np.random.permutation(np.resize(levels, 8))
        for g in range(8):
            far = levels[np.abs(levels - a[p, g]) >= 10]
            a[p, g + 8] = far[np.random.randint(len(far))]
    return np.exp2(a.ravel()).repeat(32)


def f64(x):
    return np.asarray(x).astype(np.float64)


def striped(idx):
    return np.tile(idx.reshape(-1, 16).T, (8, 1)).astype(np.uint16)


def unstriped(offs):
    return offs[:16].T.reshape(-1).astype(np.int64)


E2M1 = np.array([0.0, 0.5, 1.0, 1.5, 2.0, 3.0, 4.0, 6.0, -0.0, -0.5, -1.0, -1.5, -2.0, -3.0, -4.0, -6.0])


def pack_weight(w, fmt):
    k, n = w.shape
    w = f64(np.asarray(w, np.float32).astype(ml_dtypes.bfloat16)).reshape(k // 32, 32, n)
    amax = np.abs(w).max(1)
    if fmt == "e4m3":
        byte = np.frexp(amax)[1] - 1 + 127 - 7
    else:
        mant, ex = np.frexp(amax / 6.0)
        byte = np.where(mant > 0.5, ex, ex - 1) + 127
    byte = np.clip(np.where(amax > 0, byte, 1), 1, 254)
    scaled = (w * np.exp2(127.0 - byte)[:, None, :]).reshape(k, n).astype(np.float32)
    by_word = np.ascontiguousarray(scaled.reshape(k // 512, 128, 4, n).transpose(0, 1, 3, 2))
    if fmt == "e4m3":
        words = by_word.astype(ml_dtypes.float8_e4m3fn).view(np.uint8)
    else:
        c = by_word.astype(ml_dtypes.float4_e2m1fn).view(np.uint8) & 0xF
        words = (c[..., 0::2] | (c[..., 1::2] << 4)).reshape(k // 512, 128, 2 * n)
    return np.ascontiguousarray(words), np.ascontiguousarray(byte.astype(np.uint8).reshape(k // 512, 16, n))


def unpack_weight(words, scales, fmt):
    g, _, n = scales.shape
    words = np.ascontiguousarray(words).reshape(g, 128, n, -1)
    if fmt == "e4m3":
        vals = words.view(ml_dtypes.float8_e4m3fn).astype(np.float64)
    else:
        nib = np.empty((g, 128, n, 4), np.uint8)
        nib[..., 0::2] = words & 0xF
        nib[..., 1::2] = words >> 4
        vals = E2M1[nib]
    vals = vals * np.repeat(np.exp2(scales.astype(np.float64) - 127.0), 8, axis=1)[..., None]
    return vals.transpose(0, 1, 3, 2).reshape(g * 512, n)


def relu(v):
    return np.maximum(v, 0.0)


K, T, E, C, H, N = 512, 512, 8, 128, 512, 256


def by_expert(wq, xq):
    return np.concatenate([wq[e].T @ xq[:, e * C:(e + 1) * C] for e in range(E)], axis=1)


def setup_inputs():
    n = np.random.standard_normal
    s = mx_kscale(K)[:, None]
    u = mx_kscale(H)
    first = np.random.permutation(np.repeat(np.arange(E), T // E))
    second = (first + 1 + np.random.permutation(np.repeat(np.arange(E - 1), -(-T // (E - 1)))[:T])) % E
    while np.bincount(second, minlength=E).max() != T // E:
        load = np.bincount(second, minlength=E); hi, lo = int(load.argmax()), int(load.argmin())
        t = np.flatnonzero((second == hi) & (first != lo))[0]; second[t] = lo
    slot_token = np.empty(E * C, np.int64); pos = np.empty((2, T), np.int64); fill = np.zeros(E, np.int64)
    place = np.stack([np.random.permutation(C) for _ in range(E)])
    for r, deal in enumerate((first, second)):
        for t in np.random.permutation(T):
            e = deal[t]; j = e * C + place[e, fill[e]]; fill[e] += 1; slot_token[j] = t; pos[r, t] = j
    g = np.random.uniform(0.2, 0.8, T)
    w1 = [pack_weight(m, "e2m1") for m in n((E, K, H)) / np.sqrt(K) / s[None] * u[None, None, :]]
    w2 = [pack_weight(m, "e2m1") for m in n((E, H, N)) / np.sqrt(H) / u[None, :, None]]
    x = pack_weight(n((K, T)) * s, "e4m3")
    return {
        "x_words": x[0],
        "x_scales": x[1],
        "w1_words": np.stack([m[0] for m in w1]),
        "w1_scales": np.stack([m[1] for m in w1]),
        "w2_words": np.stack([m[0] for m in w2]),
        "w2_scales": np.stack([m[1] for m in w2]),
        "gate": np.stack([np.tile(g, (N, 1)), np.tile(1.0 - g, (N, 1))]).astype(np.float32),
        "offs": striped(slot_token),
        "pos1": striped(pos[0]),
        "pos2": striped(pos[1]),
    }


def reference(x_words, x_scales, w1_words, w1_scales, w2_words, w2_scales, gate, offs, pos1, pos2):
    idx = unstriped(offs)
    w1 = np.stack([unpack_weight(w1_words[e], w1_scales[e], "e2m1") for e in range(E)])
    w2 = np.stack([unpack_weight(w2_words[e], w2_scales[e], "e2m1") for e in range(E)])
    xq = unpack_weight(x_words, x_scales, "e4m3")[:, idx]
    h = relu(by_expert(w1, xq))
    y = by_expert(w2, mxq(h, 0, "e4m3"))
    return f64(gate[0]) * y[:, unstriped(pos1)] + f64(gate[1]) * y[:, unstriped(pos2)]

@@ -1,0 +1,229 @@
+from contextlib import ExitStack
+
+import concourse.mybir as mybir
+from concourse.masks import make_identity
+
+K, T, E, C, H, N = 512, 512, 8, 128, 512, 256
+S = E * C
+FLOPS = 2 * S * (K * H + H * N)
+
+F32 = mybir.dt.float32
+BF16 = mybir.dt.bfloat16
+I32 = mybir.dt.int32
+U32 = mybir.dt.uint32
+U16 = mybir.dt.uint16
+U8 = mybir.dt.uint8
+FP8X4 = mybir.dt.float8_e4m3fn_x4
+FP4X4 = mybir.dt.float4_e2m1fn_x4
+RELU = mybir.ActivationFunctionType.Relu
+COPY = mybir.ActivationFunctionType.Copy
+MULT = mybir.AluOpType.mult
+ADD = mybir.AluOpType.add
+
+P = 128
+GATHER_EXPERTS = [(0, 1), (1, 2), (2, 4), (4, 6), (6, 8)]
+W1_WORD_LOADS = [(0, 3), (3, 8)]
+W1_SCALE_LOADS = [(0, 3), (3, 8)]
+RELU_ON_VECTOR = (7,)
+PAIRS = E // 2
+HALF = T // 2
+
+
+def tile_moe_pkd_mlp_relu_kernel(
+    tc, x_words, x_scales, w1_words, w1_scales, w2_words, w2_scales, gate, offs, pos1, pos2, out
+):
+    nc = tc.nc
+    with ExitStack() as ctx:
+        keep = ctx.enter_context(tc.tile_pool(name="keep", bufs=1))
+        psum = ctx.enter_context(tc.psum_pool(name="psum", bufs=1))
+
+        def sb(shape, dtype, name, tag=None):
+            return keep.tile(shape, dtype, name=name, tag=tag or name, align_bytes=64)
+
+        def bank(b, shape, name):
+            return psum.tile(shape, F32, name=name, tag="bank%d" % b)
+
+        def scale_rows(plane, rows, r):
+            nc.sync.dma_start(
+                out=plane[r:P:32, :, :].bitcast(I32),
+                in_=rows[:, r:16:4, :].rearrange("e q c -> q e c").bitcast(I32),
+            )
+
+        offs_sb = keep.tile([P, S // 16], U16, name="offs_sb")
+        pos1_sb = keep.tile([P, T // 16], U16, name="pos1_sb")
+        pos2_sb = keep.tile([P, T // 16], U16, name="pos2_sb")
+        xw = sb([P, T], U32, "xw")
+        xs = sb([P, T], U8, "xs")
+        w1w = [sb([P, b - a, 2 * H], U8, "w1w%d" % a) for a, b in W1_WORD_LOADS]
+        w1s = [sb([P, b - a, H], U8, "w1s%d" % a) for a, b in W1_SCALE_LOADS]
+        w2w = sb([P, E, 2 * N], U8, "w2w")
+        w2s = sb([P, E, N], U8, "w2s")
+        gates = sb([P, 2, T], F32, "gates")
+        ident = sb([P, P], F32, "ident")
+
+        nc.vector.memset(xs[:].bitcast(I32), 0)
+        nc.vector.memset(w1s[0][:].bitcast(I32), 0)
+        nc.vector.memset(w1s[1][:].bitcast(I32), 0)
+        nc.vector.memset(w2s[:].bitcast(I32), 0)
+        make_identity(nc, ident[:])
+
+        def load_w1_words(i):
+            a, b = W1_WORD_LOADS[i]
+            nc.sync.dma_start(
+                out=w1w[i][:].bitcast(I32), in_=w1_words[a:b, 0].rearrange("e p c -> p e c").bitcast(I32)
+            )
+
+        def load_w1_scales(i):
+            a, b = W1_SCALE_LOADS[i]
+            for r in range(4):
+                scale_rows(w1s[i], w1_scales[a:b, 0], r)
+
+        nc.sync.dma_start(offs_sb[:], offs)
+        nc.sync.dma_start(out=xw[:].bitcast(I32), in_=x_words[0].rearrange("p t r -> p (t r)").bitcast(I32))
+        for r in range(4):
+            nc.sync.dma_start(out=xs[r:P:32, :].bitcast(I32), in_=x_scales[0, r:16:4, :].bitcast(I32))
+        load_w1_words(0)
+        load_w1_scales(0)
+        load_w1_words(1)
+        load_w1_scales(1)
+        nc.sync.dma_start(out=w2w[:].bitcast(I32), in_=w2_words[:, 0].rearrange("e p c -> p e c").bitcast(I32))
+        for r in range(4):
+            scale_rows(w2s, w2_scales[:, 0], r)
+        nc.sync.dma_start(pos1_sb[:], pos1)
+        nc.sync.dma_start(pos2_sb[:], pos2)
+        nc.sync.dma_start(out=gates[:], in_=gate[:, 0:P, :].rearrange("k n t -> n k t"))
+
+        slot_words, slot_scales = {}, {}
+        for a, b in GATHER_EXPERTS:
+            gw = sb([P, (b - a) * C], U32, "gw%d" % a)
+            gs = sb([P, (b - a) * C], U8, "gs%d" % a)
+            lst = offs_sb[:, a * C // 16 : b * C // 16]
+            nc.vector.tensor_copy(gw[:], xw[:].indirect(lst))
+            nc.vector.tensor_copy(gs[:], xs[:].indirect(lst))
+            for e in range(a, b):
+                slot_words[e] = gw[:, (e - a) * C : (e - a + 1) * C]
+                slot_scales[e] = gs[:, (e - a) * C : (e - a + 1) * C]
+
+        def held_by(loads, tiles, e):
+            for (a, b), t in zip(loads, tiles):
+                if a <= e < b:
+                    return t[:, e - a, :]
+
+        turned = []
+        for e in range(E):
+            acc = bank(e % 4, [P, H], "a%d" % e)
+            nc.tensor.matmul_mx(
+                out=acc[:],
+                lhsT=slot_words[e].bitcast(FP8X4),
+                lhsT_scale=slot_scales[e],
+                rhs=held_by(W1_WORD_LOADS, w1w, e).bitcast(FP4X4),
+                rhs_scale=held_by(W1_SCALE_LOADS, w1s, e),
+                start=True,
+                stop=True,
+            )
+            if e % 2 == 0:
+                hs = sb([P, 2, H], BF16, "hs%d" % (e // 2))
+            dst = hs[:, e % 2, :].rearrange("s (u p d) -> s u p d", u=2, d=2)
+            src = acc[:].rearrange("s (p u d) -> s u p d", u=2, d=2)
+            if e in RELU_ON_VECTOR:
+                nc.vector.tensor_scalar_max(dst, src, 0.0)
+            else:
+                nc.scalar.activation(dst, src, RELU)
+            if e % 2 == 1:
+                turned.append(bank(4 + e // 2, [P, 2, 2, C], "t%d" % (e // 2)))
+                words = hs[:].bitcast(F32)
+                for j in range(2):
+                    for u in range(2):
+                        nc.tensor.transpose(turned[-1][:, j, u, :], words[:, j, u * P : (u + 1) * P], ident[:])
+
+        grouped, codes, planes = {}, {}, {}
+
+        def regroup(p, on_scalar):
+            grouped[p] = sb([P, 2 * C * 4], BF16, "hq%d" % p)
+            dst = grouped[p][:].bitcast(F32).rearrange("p (j s u) -> p j s u", j=2, u=2)
+            src = turned[p][:].rearrange("p j u s -> p j s u")
+            if on_scalar:
+                nc.scalar.copy(dst, src)
+            else:
+                nc.vector.tensor_copy(dst, src)
+
+        def quantise(p):
+            tag = {0: "hs1", 1: "hs3"}.get(p)
+            codes[p] = sb([P, 2 * C], U32, "hc%d" % p, tag)
+            planes[p] = sb([P, 2 * C], U8, "hp%d" % p)
+            nc.vector.quantize_mx(out=codes[p][:].bitcast(FP8X4), scales=planes[p][:], in_=grouped[p][:])
+
+        regroup(0, False)
+        regroup(1, False)
+        regroup(2, True)
+        regroup(3, True)
+        for p in range(PAIRS):
+            quantise(p)
+
+        y = [sb([P, S], F32, "y0"), sb([P, S], F32, "y1", "hq3")]
+        y_banks = [(2, 3), (0, 1), (4, 5), (6, 7)]
+        for p in range(PAIRS):
+            for b in range(2):
+                acc = bank(y_banks[p][b], [P, 2 * C], "y%d_%d" % (p, b))
+                for j in range(2):
+                    e = 2 * p + j
+                    nc.tensor.matmul_mx(
+                        out=acc[:, j * C : (j + 1) * C],
+                        lhsT=w2w[:, e, 2 * P * b : 2 * P * (b + 1)].bitcast(FP4X4),
+                        lhsT_scale=w2s[:, e, P * b : P * (b + 1)],
+                        rhs=codes[p][:, j * C : (j + 1) * C].bitcast(FP8X4),
+                        rhs_scale=planes[p][:, j * C : (j + 1) * C],
+                        start=True,
+                        stop=True,
+                    )
+                dst = y[b][:, 2 * C * p : 2 * C * (p + 1)]
+                if b == 0 or p == PAIRS - 1:
+                    nc.scalar.copy(dst, acc[:])
+                else:
+                    nc.vector.tensor_copy(dst, acc[:])
+
+        lists = (pos1_sb, pos2_sb)
+        weighted = {}
+
+        def window(b, h, k):
+            return y[b][:].indirect(lists[k][:, h * HALF // 16 : (h + 1) * HALF // 16])
+
+        def gate_of(h, k):
+            return gates[:, k, h * HALF : (h + 1) * HALF]
+
+        def fused(b, h, k):
+            weighted[b, h, k] = sb([P, HALF], F32, "w%d%d%d" % (b, h, k))
+            nc.vector.tensor_tensor(weighted[b, h, k][:], window(b, h, k), gate_of(h, k), MULT)
+
+        fetched = {}
+
+        def fetch(b, h, k):
+            fetched[b, h, k] = sb([P, HALF], F32, "f%d%d%d" % (b, h, k))
+            nc.scalar.activation(fetched[b, h, k][:], window(b, h, k), COPY)
+
+        def weigh(b, h, k):
+            weighted[b, h, k] = sb([P, HALF], F32, "w%d%d%d" % (b, h, k))
+            nc.vector.tensor_tensor(weighted[b, h, k][:], fetched[b, h, k][:], gate_of(h, k), MULT)
+
+        def finish(b, h):
+            res = sb([P, HALF], F32, "o%d%d" % (b, h))
+            nc.vector.tensor_tensor(res[:], weighted[b, h, 0][:], weighted[b, h, 1][:], ADD)
+            nc.sync.dma_start(out=out[b * P : (b + 1) * P, h * HALF : (h + 1) * HALF], in_=res[:])
+
+        fetch(0, 0, 1)
+        fetch(0, 1, 1)
+        for h in range(2):
+            fetch(1, h, 1)
+            fetch(1, h, 0)
+        fused(0, 0, 0)
+        fused(0, 1, 0)
+        weigh(0, 0, 1)
+        weigh(0, 1, 1)
+        finish(0, 0)
+        weigh(1, 0, 1)
+        finish(0, 1)
+        weigh(1, 0, 0)
+        weigh(1, 1, 1)
+        weigh(1, 1, 0)
+        finish(1, 0)
+        finish(1, 1)

@@ -21,10 +21,11 @@ MULT = mybir.AluOpType.mult
 ADD = mybir.AluOpType.add
 
 P = 128
-GATHER_EXPERTS = [(0, 1), (1, 2), (2, 4), (4, 6), (6, 8)]
-W1_WORD_LOADS = [(0, 3), (3, 8)]
-W1_SCALE_LOADS = [(0, 3), (3, 8)]
-RELU_ON_VECTOR = (7,)
+GATHER_EXPERTS = [(0, 2), (2, 4), (4, 6), (6, 8)]
+W1_WORD_LOADS = [(0, 4), (4, 8)]
+W1_SCALE_LOADS = [(0, 4), (4, 8)]
+RELU_ON_VECTOR = (6, 7)
+TURNS = [(0, 2, 0, True), (2, 4, 2, False), (4, 6, 4, False), (6, 7, 5, True), (7, 8, 2, False)]
 PAIRS = E // 2
 HALF = T // 2
 
@@ -61,11 +62,14 @@ def tile_moe_pkd_mlp_relu_kernel(
         gates = sb([P, 2, T], F32, "gates")
         ident = sb([P, P], F32, "ident")
 
-        nc.vector.memset(xs[:].bitcast(I32), 0)
+        nc.gpsimd.memset(xs[:].bitcast(I32), 0)
         nc.vector.memset(w1s[0][:].bitcast(I32), 0)
         nc.vector.memset(w1s[1][:].bitcast(I32), 0)
         nc.vector.memset(w2s[:].bitcast(I32), 0)
         make_identity(nc, ident[:])
+
+        def load_x_scales(r):
+            nc.sync.dma_start(out=xs[r:P:32, :].bitcast(I32), in_=x_scales[0, r:16:4, :].bitcast(I32))
 
         def load_w1_words(i):
             a, b = W1_WORD_LOADS[i]
@@ -73,23 +77,23 @@ def tile_moe_pkd_mlp_relu_kernel(
                 out=w1w[i][:].bitcast(I32), in_=w1_words[a:b, 0].rearrange("e p c -> p e c").bitcast(I32)
             )
 
-        def load_w1_scales(i):
+        def load_w1_scales(i, rows):
             a, b = W1_SCALE_LOADS[i]
-            for r in range(4):
+            for r in rows:
                 scale_rows(w1s[i], w1_scales[a:b, 0], r)
 
-        nc.sync.dma_start(offs_sb[:], offs)
-        nc.sync.dma_start(out=xw[:].bitcast(I32), in_=x_words[0].rearrange("p t r -> p (t r)").bitcast(I32))
+        nc.sync.dma_start(pos1_sb[:], pos1)
         for r in range(4):
-            nc.sync.dma_start(out=xs[r:P:32, :].bitcast(I32), in_=x_scales[0, r:16:4, :].bitcast(I32))
+            load_x_scales(r)
+        nc.sync.dma_start(out=xw[:].bitcast(I32), in_=x_words[0].rearrange("p t r -> p (t r)").bitcast(I32))
+        nc.sync.dma_start(offs_sb[:], offs)
         load_w1_words(0)
-        load_w1_scales(0)
+        load_w1_scales(0, range(4))
         load_w1_words(1)
-        load_w1_scales(1)
+        load_w1_scales(1, range(4))
         nc.sync.dma_start(out=w2w[:].bitcast(I32), in_=w2_words[:, 0].rearrange("e p c -> p e c").bitcast(I32))
         for r in range(4):
             scale_rows(w2s, w2_scales[:, 0], r)
-        nc.sync.dma_start(pos1_sb[:], pos1)
         nc.sync.dma_start(pos2_sb[:], pos2)
         nc.sync.dma_start(out=gates[:], in_=gate[:, 0:P, :].rearrange("k n t -> n k t"))
 
@@ -109,9 +113,10 @@ def tile_moe_pkd_mlp_relu_kernel(
                 if a <= e < b:
                     return t[:, e - a, :]
 
-        turned = []
-        for e in range(E):
-            acc = bank(e % 4, [P, H], "a%d" % e)
+        hidden, turned = {}, {}
+
+        def first_layer(e):
+            acc = bank(e, [P, H], "a%d" % e)
             nc.tensor.matmul_mx(
                 out=acc[:],
                 lhsT=slot_words[e].bitcast(FP8X4),
@@ -121,109 +126,104 @@ def tile_moe_pkd_mlp_relu_kernel(
                 start=True,
                 stop=True,
             )
-            if e % 2 == 0:
-                hs = sb([P, 2, H], BF16, "hs%d" % (e // 2))
-            dst = hs[:, e % 2, :].rearrange("s (u p d) -> s u p d", u=2, d=2)
+            if e >= E - 2:
+                hidden[e] = sb([P, H], BF16, "hs_last%d" % e)[:]
+            elif e % 2 == 0:
+                both = sb([P, 2, H], BF16, "hs%d" % (e // 2))
+                hidden[e], hidden[e + 1] = both[:, 0, :], both[:, 1, :]
+            dst = hidden[e].rearrange("s (u p d) -> s u p d", u=2, d=2)
             src = acc[:].rearrange("s (p u d) -> s u p d", u=2, d=2)
             if e in RELU_ON_VECTOR:
                 nc.vector.tensor_scalar_max(dst, src, 0.0)
             else:
                 nc.scalar.activation(dst, src, RELU)
-            if e % 2 == 1:
-                turned.append(bank(4 + e // 2, [P, 2, 2, C], "t%d" % (e // 2)))
-                words = hs[:].bitcast(F32)
-                for j in range(2):
-                    for u in range(2):
-                        nc.tensor.transpose(turned[-1][:, j, u, :], words[:, j, u * P : (u + 1) * P], ident[:])
 
-        grouped, codes, planes = {}, {}, {}
+        def turn(first, last, b):
+            turned[first] = bank(b, [P, last - first, 2, C], "t%d" % first)
+            for e in range(first, last):
+                words = hidden[e].bitcast(F32)
+                for u in range(2):
+                    nc.tensor.transpose(turned[first][:, e - first, u, :], words[:, u * P : (u + 1) * P], ident[:])
 
-        def regroup(p, on_scalar):
-            grouped[p] = sb([P, 2 * C * 4], BF16, "hq%d" % p)
-            dst = grouped[p][:].bitcast(F32).rearrange("p (j s u) -> p j s u", j=2, u=2)
-            src = turned[p][:].rearrange("p j u s -> p j s u")
-            if on_scalar:
-                nc.scalar.copy(dst, src)
-            else:
+        for e in range(E):
+            first_layer(e)
+        for first, last, b, on_vector in TURNS:
+            turn(first, last, b)
+
+        grouped = [sb([P, 2 * C * 4], BF16, "hq%d" % p) for p in range(PAIRS)]
+        for first, last, b, on_vector in TURNS:
+            dst = grouped[first // 2][:].bitcast(F32).rearrange("p (j s u) -> p j s u", j=2, u=2)
+            dst = dst[:, first % 2 : first % 2 + last - first]
+            src = turned[first][:].rearrange("p j u s -> p j s u")
+            if on_vector:
                 nc.vector.tensor_copy(dst, src)
+            else:
+                nc.scalar.copy(dst, src)
 
-        def quantise(p):
-            tag = {0: "hs1", 1: "hs3"}.get(p)
-            codes[p] = sb([P, 2 * C], U32, "hc%d" % p, tag)
-            planes[p] = sb([P, 2 * C], U8, "hp%d" % p)
+        codes, planes = [], []
+        for p in range(PAIRS):
+            codes.append(sb([P, 2 * C], U32, "hc%d" % p, {0: "w1s4", 2: "hs_last7"}.get(p)))
+            planes.append(sb([P, 2 * C], U8, "hp%d" % p))
             nc.vector.quantize_mx(out=codes[p][:].bitcast(FP8X4), scales=planes[p][:], in_=grouped[p][:])
 
-        regroup(0, False)
-        regroup(1, False)
-        regroup(2, True)
-        regroup(3, True)
-        for p in range(PAIRS):
-            quantise(p)
-
         y = [sb([P, S], F32, "y0"), sb([P, S], F32, "y1", "hq3")]
-        y_banks = [(2, 3), (0, 1), (4, 5), (6, 7)]
-        for p in range(PAIRS):
+        groups = [(0, 4), (4, 6), (6, 8)]
+        y_banks = [(1, 3), (6, 0), (7, 4)]
+        for g, (first, last) in enumerate(groups):
             for b in range(2):
-                acc = bank(y_banks[p][b], [P, 2 * C], "y%d_%d" % (p, b))
-                for j in range(2):
-                    e = 2 * p + j
+                acc = bank(y_banks[g][b], [P, (last - first) * C], "y%d_%d" % (b, g))
+                for e in range(first, last):
+                    cols = slice((e % 2) * C, (e % 2 + 1) * C)
                     nc.tensor.matmul_mx(
-                        out=acc[:, j * C : (j + 1) * C],
+                        out=acc[:, (e - first) * C : (e - first + 1) * C],
                         lhsT=w2w[:, e, 2 * P * b : 2 * P * (b + 1)].bitcast(FP4X4),
                         lhsT_scale=w2s[:, e, P * b : P * (b + 1)],
-                        rhs=codes[p][:, j * C : (j + 1) * C].bitcast(FP8X4),
-                        rhs_scale=planes[p][:, j * C : (j + 1) * C],
+                        rhs=codes[e // 2][:, cols].bitcast(FP8X4),
+                        rhs_scale=planes[e // 2][:, cols],
                         start=True,
                         stop=True,
                     )
-                dst = y[b][:, 2 * C * p : 2 * C * (p + 1)]
-                if b == 0 or p == PAIRS - 1:
+                dst = y[b][:, first * C : last * C]
+                if b == 1 and g < 2:
+                    nc.vector.tensor_copy(dst, acc[:])
+                elif b == 0:
                     nc.scalar.copy(dst, acc[:])
                 else:
-                    nc.vector.tensor_copy(dst, acc[:])
+                    last_copy = (dst, acc)
 
         lists = (pos1_sb, pos2_sb)
-        weighted = {}
+        fetched = [sb([P, 2, T], F32, "fetched%d" % b) for b in range(2)]
+        weighted = [sb([P, 2, T], F32, "weighted%d" % b) for b in range(2)]
+        result = [sb([P, T], F32, "result%d" % b) for b in range(2)]
+        whole, low, high = slice(0, T), slice(0, HALF), slice(HALF, T)
 
-        def window(b, h, k):
-            return y[b][:].indirect(lists[k][:, h * HALF // 16 : (h + 1) * HALF // 16])
+        def window(b, k, t):
+            return y[b][:].indirect(lists[k][:, t.start // 16 : t.stop // 16])
 
-        def gate_of(h, k):
-            return gates[:, k, h * HALF : (h + 1) * HALF]
+        def fused(b, k, t):
+            nc.vector.tensor_tensor(weighted[b][:, k, t], window(b, k, t), gates[:, k, t], MULT)
 
-        def fused(b, h, k):
-            weighted[b, h, k] = sb([P, HALF], F32, "w%d%d%d" % (b, h, k))
-            nc.vector.tensor_tensor(weighted[b, h, k][:], window(b, h, k), gate_of(h, k), MULT)
+        def fetch(b, k, t):
+            nc.scalar.activation(fetched[b][:, k, t], window(b, k, t), COPY)
 
-        fetched = {}
+        def weigh(b, k, t):
+            nc.vector.tensor_tensor(weighted[b][:, k, t], fetched[b][:, k, t], gates[:, k, t], MULT)
 
-        def fetch(b, h, k):
-            fetched[b, h, k] = sb([P, HALF], F32, "f%d%d%d" % (b, h, k))
-            nc.scalar.activation(fetched[b, h, k][:], window(b, h, k), COPY)
+        def finish(b, t):
+            nc.vector.tensor_tensor(result[b][:, t], weighted[b][:, 0, t], weighted[b][:, 1, t], ADD)
+            nc.sync.dma_start(out=out[b * P : (b + 1) * P, t], in_=result[b][:, t])
 
-        def weigh(b, h, k):
-            weighted[b, h, k] = sb([P, HALF], F32, "w%d%d%d" % (b, h, k))
-            nc.vector.tensor_tensor(weighted[b, h, k][:], fetched[b, h, k][:], gate_of(h, k), MULT)
-
-        def finish(b, h):
-            res = sb([P, HALF], F32, "o%d%d" % (b, h))
-            nc.vector.tensor_tensor(res[:], weighted[b, h, 0][:], weighted[b, h, 1][:], ADD)
-            nc.sync.dma_start(out=out[b * P : (b + 1) * P, h * HALF : (h + 1) * HALF], in_=res[:])
-
-        fetch(0, 0, 1)
-        fetch(0, 1, 1)
-        for h in range(2):
-            fetch(1, h, 1)
-            fetch(1, h, 0)
-        fused(0, 0, 0)
-        fused(0, 1, 0)
-        weigh(0, 0, 1)
-        weigh(0, 1, 1)
-        finish(0, 0)
-        weigh(1, 0, 1)
-        finish(0, 1)
-        weigh(1, 0, 0)
-        weigh(1, 1, 1)
-        weigh(1, 1, 0)
-        finish(1, 0)
-        finish(1, 1)
+        fetch(0, 1, whole)
+        nc.scalar.copy(last_copy[0], last_copy[1][:])
+        for t in (low, high):
+            fetch(1, 1, t)
+            fetch(1, 0, t)
+        fused(0, 0, whole)
+        weigh(0, 1, whole)
+        weigh(1, 1, low)
+        finish(0, whole)
+        weigh(1, 0, low)
+        weigh(1, 1, high)
+        weigh(1, 0, high)
+        finish(1, low)
+        finish(1, high)

from contextlib import ExitStack

import concourse.mybir as mybir
from concourse.masks import make_identity

K, T, E, C, H, N = 512, 512, 8, 128, 512, 256
S = E * C
FLOPS = 2 * S * (K * H + H * N)

F32 = mybir.dt.float32
BF16 = mybir.dt.bfloat16
I32 = mybir.dt.int32
U32 = mybir.dt.uint32
U16 = mybir.dt.uint16
U8 = mybir.dt.uint8
FP8X4 = mybir.dt.float8_e4m3fn_x4
FP4X4 = mybir.dt.float4_e2m1fn_x4
RELU = mybir.ActivationFunctionType.Relu
COPY = mybir.ActivationFunctionType.Copy
MULT = mybir.AluOpType.mult
ADD = mybir.AluOpType.add

P = 128
GATHER_EXPERTS = [(0, 2), (2, 4), (4, 6), (6, 8)]
W1_WORD_LOADS = [(0, 4), (4, 8)]
W1_SCALE_LOADS = [(0, 4), (4, 8)]
RELU_ON_VECTOR = (6, 7)
TURNS = [(0, 2, 0, True), (2, 4, 2, False), (4, 6, 4, False), (6, 7, 5, True), (7, 8, 2, False)]
PAIRS = E // 2
HALF = T // 2


def tile_moe_pkd_mlp_relu_kernel(
    tc, x_words, x_scales, w1_words, w1_scales, w2_words, w2_scales, gate, offs, pos1, pos2, out
):
    nc = tc.nc
    with ExitStack() as ctx:
        keep = ctx.enter_context(tc.tile_pool(name="keep", bufs=1))
        psum = ctx.enter_context(tc.psum_pool(name="psum", bufs=1))

        def sb(shape, dtype, name, tag=None):
            return keep.tile(shape, dtype, name=name, tag=tag or name, align_bytes=64)

        def bank(b, shape, name):
            return psum.tile(shape, F32, name=name, tag="bank%d" % b)

        def scale_rows(plane, rows, r):
            nc.sync.dma_start(
                out=plane[r:P:32, :, :].bitcast(I32),
                in_=rows[:, r:16:4, :].rearrange("e q c -> q e c").bitcast(I32),
            )

        offs_sb = keep.tile([P, S // 16], U16, name="offs_sb")
        pos1_sb = keep.tile([P, T // 16], U16, name="pos1_sb")
        pos2_sb = keep.tile([P, T // 16], U16, name="pos2_sb")
        xw = sb([P, T], U32, "xw")
        xs = sb([P, T], U8, "xs")
        w1w = [sb([P, b - a, 2 * H], U8, "w1w%d" % a) for a, b in W1_WORD_LOADS]
        w1s = [sb([P, b - a, H], U8, "w1s%d" % a) for a, b in W1_SCALE_LOADS]
        w2w = sb([P, E, 2 * N], U8, "w2w")
        w2s = sb([P, E, N], U8, "w2s")
        gates = sb([P, 2, T], F32, "gates")
        ident = sb([P, P], F32, "ident")

        nc.gpsimd.memset(xs[:].bitcast(I32), 0)
        nc.vector.memset(w1s[0][:].bitcast(I32), 0)
        nc.vector.memset(w1s[1][:].bitcast(I32), 0)
        nc.vector.memset(w2s[:].bitcast(I32), 0)
        make_identity(nc, ident[:])

        def load_x_scales(r):
            nc.sync.dma_start(out=xs[r:P:32, :].bitcast(I32), in_=x_scales[0, r:16:4, :].bitcast(I32))

        def load_w1_words(i):
            a, b = W1_WORD_LOADS[i]
            nc.sync.dma_start(
                out=w1w[i][:].bitcast(I32), in_=w1_words[a:b, 0].rearrange("e p c -> p e c").bitcast(I32)
            )

        def load_w1_scales(i, rows):
            a, b = W1_SCALE_LOADS[i]
            for r in rows:
                scale_rows(w1s[i], w1_scales[a:b, 0], r)

        nc.sync.dma_start(pos1_sb[:], pos1)
        for r in range(4):
            load_x_scales(r)
        nc.sync.dma_start(out=xw[:].bitcast(I32), in_=x_words[0].rearrange("p t r -> p (t r)").bitcast(I32))
        nc.sync.dma_start(offs_sb[:], offs)
        load_w1_words(0)
        load_w1_scales(0, range(4))
        load_w1_words(1)
        load_w1_scales(1, range(4))
        nc.sync.dma_start(out=w2w[:].bitcast(I32), in_=w2_words[:, 0].rearrange("e p c -> p e c").bitcast(I32))
        for r in range(4):
            scale_rows(w2s, w2_scales[:, 0], r)
        nc.sync.dma_start(pos2_sb[:], pos2)
        nc.sync.dma_start(out=gates[:], in_=gate[:, 0:P, :].rearrange("k n t -> n k t"))

        slot_words, slot_scales = {}, {}
        for a, b in GATHER_EXPERTS:
            gw = sb([P, (b - a) * C], U32, "gw%d" % a)
            gs = sb([P, (b - a) * C], U8, "gs%d" % a)
            lst = offs_sb[:, a * C // 16 : b * C // 16]
            nc.vector.tensor_copy(gw[:], xw[:].indirect(lst))
            nc.vector.tensor_copy(gs[:], xs[:].indirect(lst))
            for e in range(a, b):
                slot_words[e] = gw[:, (e - a) * C : (e - a + 1) * C]
                slot_scales[e] = gs[:, (e - a) * C : (e - a + 1) * C]

        def held_by(loads, tiles, e):
            for (a, b), t in zip(loads, tiles):
                if a <= e < b:
                    return t[:, e - a, :]

        hidden, turned = {}, {}

        def first_layer(e):
            acc = bank(e, [P, H], "a%d" % e)
            nc.tensor.matmul_mx(
                out=acc[:],
                lhsT=slot_words[e].bitcast(FP8X4),
                lhsT_scale=slot_scales[e],
                rhs=held_by(W1_WORD_LOADS, w1w, e).bitcast(FP4X4),
                rhs_scale=held_by(W1_SCALE_LOADS, w1s, e),
                start=True,
                stop=True,
            )
            if e >= E - 2:
                hidden[e] = sb([P, H], BF16, "hs_last%d" % e)[:]
            elif e % 2 == 0:
                both = sb([P, 2, H], BF16, "hs%d" % (e // 2))
                hidden[e], hidden[e + 1] = both[:, 0, :], both[:, 1, :]
            dst = hidden[e].rearrange("s (u p d) -> s u p d", u=2, d=2)
            src = acc[:].rearrange("s (p u d) -> s u p d", u=2, d=2)
            if e in RELU_ON_VECTOR:
                nc.vector.tensor_scalar_max(dst, src, 0.0)
            else:
                nc.scalar.activation(dst, src, RELU)

        def turn(first, last, b):
            turned[first] = bank(b, [P, last - first, 2, C], "t%d" % first)
            for e in range(first, last):
                words = hidden[e].bitcast(F32)
                for u in range(2):
                    nc.tensor.transpose(turned[first][:, e - first, u, :], words[:, u * P : (u + 1) * P], ident[:])

        for e in range(E):
            first_layer(e)
        for first, last, b, on_vector in TURNS:
            turn(first, last, b)

        grouped = [sb([P, 2 * C * 4], BF16, "hq%d" % p) for p in range(PAIRS)]
        for first, last, b, on_vector in TURNS:
            dst = grouped[first // 2][:].bitcast(F32).rearrange("p (j s u) -> p j s u", j=2, u=2)
            dst = dst[:, first % 2 : first % 2 + last - first]
            src = turned[first][:].rearrange("p j u s -> p j s u")
            if on_vector:
                nc.vector.tensor_copy(dst, src)
            else:
                nc.scalar.copy(dst, src)

        codes, planes = [], []
        for p in range(PAIRS):
            codes.append(sb([P, 2 * C], U32, "hc%d" % p, {0: "w1s4", 2: "hs_last7"}.get(p)))
            planes.append(sb([P, 2 * C], U8, "hp%d" % p))
            nc.vector.quantize_mx(out=codes[p][:].bitcast(FP8X4), scales=planes[p][:], in_=grouped[p][:])

        y = [sb([P, S], F32, "y0"), sb([P, S], F32, "y1", "hq3")]
        groups = [(0, 4), (4, 6), (6, 8)]
        y_banks = [(1, 3), (6, 0), (7, 4)]
        for g, (first, last) in enumerate(groups):
            for b in range(2):
                acc = bank(y_banks[g][b], [P, (last - first) * C], "y%d_%d" % (b, g))
                for e in range(first, last):
                    cols = slice((e % 2) * C, (e % 2 + 1) * C)
                    nc.tensor.matmul_mx(
                        out=acc[:, (e - first) * C : (e - first + 1) * C],
                        lhsT=w2w[:, e, 2 * P * b : 2 * P * (b + 1)].bitcast(FP4X4),
                        lhsT_scale=w2s[:, e, P * b : P * (b + 1)],
                        rhs=codes[e // 2][:, cols].bitcast(FP8X4),
                        rhs_scale=planes[e // 2][:, cols],
                        start=True,
                        stop=True,
                    )
                dst = y[b][:, first * C : last * C]
                if b == 1 and g < 2:
                    nc.vector.tensor_copy(dst, acc[:])
                elif b == 0:
                    nc.scalar.copy(dst, acc[:])
                else:
                    last_copy = (dst, acc)

        lists = (pos1_sb, pos2_sb)
        fetched = [sb([P, 2, T], F32, "fetched%d" % b) for b in range(2)]
        weighted = [sb([P, 2, T], F32, "weighted%d" % b) for b in range(2)]
        result = [sb([P, T], F32, "result%d" % b) for b in range(2)]
        whole, low, high = slice(0, T), slice(0, HALF), slice(HALF, T)

        def window(b, k, t):
            return y[b][:].indirect(lists[k][:, t.start // 16 : t.stop // 16])

        def fused(b, k, t):
            nc.vector.tensor_tensor(weighted[b][:, k, t], window(b, k, t), gates[:, k, t], MULT)

        def fetch(b, k, t):
            nc.scalar.activation(fetched[b][:, k, t], window(b, k, t), COPY)

        def weigh(b, k, t):
            nc.vector.tensor_tensor(weighted[b][:, k, t], fetched[b][:, k, t], gates[:, k, t], MULT)

        def finish(b, t):
            nc.vector.tensor_tensor(result[b][:, t], weighted[b][:, 0, t], weighted[b][:, 1, t], ADD)
            nc.sync.dma_start(out=out[b * P : (b + 1) * P, t], in_=result[b][:, t])

        fetch(0, 1, whole)
        nc.scalar.copy(last_copy[0], last_copy[1][:])
        for t in (low, high):
            fetch(1, 1, t)
            fetch(1, 0, t)
        fused(0, 0, whole)
        weigh(0, 1, whole)
        weigh(1, 1, low)
        finish(0, whole)
        weigh(1, 0, low)
        weigh(1, 1, high)
        weigh(1, 0, high)
        finish(1, low)
        finish(1, high)
